import numpy as np
import ml_dtypes


def mxq(x, axis, fmt="e4m3"):
    dtype, down = {"e4m3": (ml_dtypes.float8_e4m3fn, 7), "e5m2": (ml_dtypes.float8_e5m2, 14)}[fmt]
    v = np.moveaxis(np.asarray(x, np.float32).astype(ml_dtypes.bfloat16).astype(np.float64), axis, -1)
    blocks = v.reshape(v.shape[:-1] + (-1, 32))
    amax = np.abs(blocks).max(-1, keepdims=True)
    byte = np.maximum(np.where(amax > 0, np.frexp(amax)[1] - 1 + 127, 0) - down, 1)
    scale = np.exp2(byte - 127.0)
    codes = (blocks / scale).astype(np.float32).astype(dtype).astype(np.float64)
    return np.moveaxis((codes * scale).reshape(v.shape), -1, axis)


WIDE = False


def mx_kscale(k):
    if not WIDE:
        return np.ones(k)
    levels = np.array([10, -10, 5, -5, 0])
    if k % 512:
        return np.exp2(np.random.permutation(np.resize(levels, k // 32))).repeat(32)
    a = np.empty((k // 512, 16))
    for p in range(k // 512):
        a[p, :8] = np.random.permutation(np.resize(levels, 8))
        for g in range(8):
            far = levels[np.abs(levels - a[p, g]) >= 10]
            a[p, g + 8] = far[np.random.randint(len(far))]
    return np.exp2(a.ravel()).repeat(32)


def f64(x):
    return np.asarray(x).astype(np.float64)


def striped(idx):
    return np.tile(idx.reshape(-1, 16).T, (8, 1)).astype(np.uint16)


def unstriped(offs):
    return offs[:16].T.reshape(-1).astype(np.int64)


E2M1 = np.array([0.0, 0.5, 1.0, 1.5, 2.0, 3.0, 4.0, 6.0, -0.0, -0.5, -1.0, -1.5, -2.0, -3.0, -4.0, -6.0])


def pack_weight(w, fmt):
    k, n = w.shape
    w = f64(np.asarray(w, np.float32).astype(ml_dtypes.bfloat16)).reshape(k // 32, 32, n)
    amax = np.abs(w).max(1)
    if fmt == "e4m3":
        byte = np.frexp(amax)[1] - 1 + 127 - 7
    else:
        mant, ex = np.frexp(amax / 6.0)
        byte = np.where(mant > 0.5, ex, ex - 1) + 127
    byte = np.clip(np.where(amax > 0, byte, 1), 1, 254)
    scaled = (w * np.exp2(127.0 - byte)[:, None, :]).reshape(k, n).astype(np.float32)
    by_word = np.ascontiguousarray(scaled.reshape(k // 512, 128, 4, n).transpose(0, 1, 3, 2))
    if fmt == "e4m3":
        words = by_word.astype(ml_dtypes.float8_e4m3fn).view(np.uint8)
    else:
        c = by_word.astype(ml_dtypes.float4_e2m1fn).view(np.uint8) & 0xF
        words = (c[..., 0::2] | (c[..., 1::2] << 4)).reshape(k // 512, 128, 2 * n)
    return np.ascontiguousarray(words), np.ascontiguousarray(byte.astype(np.uint8).reshape(k // 512, 16, n))


def unpack_weight(words, scales, fmt):
    g, _, n = scales.shape
    words = np.ascontiguousarray(words).reshape(g, 128, n, -1)
    if fmt == "e4m3":
        vals = words.view(ml_dtypes.float8_e4m3fn).astype(np.float64)
    else:
        nib = np.empty((g, 128, n, 4), np.uint8)
        nib[..., 0::2] = words & 0xF
        nib[..., 1::2] = words >> 4
        vals = E2M1[nib]
    vals = vals * np.repeat(np.exp2(scales.astype(np.float64) - 127.0), 8, axis=1)[..., None]
    return vals.transpose(0, 1, 3, 2).reshape(g * 512, n)


def gelu(v):
    return 0.5 * v * (1.0 + np.tanh(np.sqrt(2.0 / np.pi) * (v + 0.044715 * v**3)))


K, T, S, S2 = 1024, 4096, 1024, 512


def setup_inputs():
    n = np.random.standard_normal
    s = mx_kscale(K)[:, None]
    d = {}
    loud = np.exp(0.3 * n(T))
    d["tab_words"], d["tab_scales"] = pack_weight(n((K, T)) * loud * s, "e4m3")
    d["offs"] = striped(np.random.permutation(T)[:S])
    d["offs2"] = striped(np.random.permutation(T)[:S2])
    d["w1"] = (1.3 * n((K, K)) / K / s / s.T).astype(np.float32)
    w2 = 1.3 * n((K, K)) / K / s / s.T
    d["w2_words"], d["w2_scales"] = pack_weight(w2, "e2m1")
    return d


def reference(tab_words, tab_scales, offs, offs2, w1, w2_words, w2_scales):
    TW = unpack_weight(tab_words, tab_scales, "e4m3")
    v = TW[:, unstriped(offs)]
    v2 = TW[:, unstriped(offs2)]
    w1q = mxq(f64(w1), 0, "e4m3")
    w2 = unpack_weight(w2_words, w2_scales, "e2m1")
    c1 = w1q.T @ v
    c2 = w2.T @ v
    h = np.sqrt(np.square(c1) + np.square(c2))
    hq = mxq(h, 0, "e4m3")
    e = v2.T @ hq
    return np.log(1.0 + np.square(e))

@@ -1,0 +1,254 @@
+from contextlib import ExitStack
+
+import concourse.mybir as mybir
+
+K, T, S, S2 = 1024, 4096, 1024, 512
+FLOPS = 2 * (2 * K * K * S + K * S2 * S)
+
+F32 = mybir.dt.float32
+BF16 = mybir.dt.bfloat16
+I32 = mybir.dt.int32
+U32 = mybir.dt.uint32
+U16 = mybir.dt.uint16
+U8 = mybir.dt.uint8
+FP8X4 = mybir.dt.float8_e4m3fn_x4
+FP4X4 = mybir.dt.float4_e2m1fn_x4
+ACT = mybir.ActivationFunctionType
+ALU = mybir.AluOpType
+
+P = 128
+PACK = 4
+KP = P * PACK
+PASSES = K // KP
+QUADS = 4
+NQ = 256
+QS = S // NQ
+MT = S2 // P
+
+
+def tile_list_gear_whine_pairs_kernel(tc, tab_words, tab_scales, offs, offs2, w1, w2_words, w2_scales, out):
+    nc = tc.nc
+    with ExitStack() as ctx:
+        lists = ctx.enter_context(tc.tile_pool(name="lists", bufs=1))
+        keep = ctx.enter_context(tc.tile_pool(name="keep", bufs=1))
+        ring = ctx.enter_context(tc.tile_pool(name="ring", bufs=2))
+        ring3 = ctx.enter_context(tc.tile_pool(name="ring3", bufs=3))
+        stage = ctx.enter_context(tc.tile_pool(name="stage", bufs=1))
+        psum = ctx.enter_context(tc.psum_pool(name="psum", bufs=1))
+
+        def held(name, shape, dtype):
+            return keep.tile(shape, dtype, name=name, align_bytes=64)
+
+        def bank(n):
+            return psum.tile([P, 2, NQ], F32, name="bank%d" % n)
+
+        idx = lists.tile([P, S // 16], U16, name="idx")
+        idx2 = lists.tile([P, S2 // 16], U16, name="idx2")
+        chunk = 4 * PACK * KP
+
+        def staged(name, shape, dtype, offset):
+            return stage.tile(shape, dtype, name=name, offset=offset, align_bytes=64)
+
+        tab_s = staged("tab_s", [P, T], U8, 5 * chunk - T // 2)
+        w2s_raw = held("w2s_raw", [P, PASSES * K], U8)
+        vs_hi = held("vs_hi", [P, S], U8)
+        nc.vector.memset(tab_s[:].bitcast(I32), 0)
+        nc.vector.memset(w2s_raw[:].bitcast(I32), 0)
+        nc.vector.memset(vs_hi[:].bitcast(I32), 0)
+
+        w2w_raw = {}
+        for b in range(PASSES):
+            for a in range(PASSES):
+                t = staged("w2w_raw%d%d" % (a, b), [P, 2 * KP], U8, 2 * a * chunk if b == 0 else (6 * chunk + 2 * KP * a))
+                nc.sync.dma_start(t[:].bitcast(I32), w2_words[a, :, 2 * KP * b : 2 * KP * (b + 1)].bitcast(I32))
+                w2w_raw[a, b] = t
+        nc.sync.dma_start(idx[:], offs)
+        nc.sync.dma_start(idx2[:], offs2)
+        for q in range(QUADS):
+            nc.sync.dma_start(tab_s[32 * q : 32 * q + 8, :].bitcast(I32), tab_scales[:, 4 * q : 4 * q + 4, :].bitcast(I32))
+        for q in range(QUADS):
+            nc.sync.dma_start(
+                w2s_raw[32 * q : 32 * q + 4, :].bitcast(I32).rearrange("r (a c) -> r a c", a=PASSES),
+                w2_scales[:, 4 * q : 4 * q + 4, :].rearrange("a r c -> r a c").bitcast(I32),
+            )
+        w2w = held("w2w", [P, PASSES * 2 * K], U8)
+        for b in range(PASSES):
+            for a in range(PASSES):
+                c0 = 2 * (K * a + KP * b)
+                nc.scalar.copy(
+                    w2w[:, c0 : c0 + 2 * KP].bitcast(U16).rearrange("p (i m) -> p i m", i=PACK),
+                    w2w_raw[a, b][:].bitcast(U16).rearrange("p (m i) -> p i m", i=PACK),
+                )
+        tab_w = []
+        for a in range(PASSES):
+            t = staged("tab_w%d" % a, [P, T], U32, 2 * a * chunk)
+            nc.sync.dma_start(t[:].bitcast(I32), tab_words[a].rearrange("p t i -> p (t i)").bitcast(I32))
+            tab_w.append(t)
+        vs_lo = held("vs_lo", [P, S], U8)
+        nc.vector.tensor_copy(vs_lo[:], tab_s[:].indirect(idx[:]))
+        nc.scalar.dma_start(vs_hi[0:100, :].bitcast(I32), vs_lo[4:104, :].bitcast(I32))
+        vs = [vs_lo, vs_hi]
+        vw = [held("vw%d" % a, [P, S], U32) for a in range(PASSES)]
+        v2w = [held("v2w%d" % a, [P, S2], U32) for a in range(PASSES)]
+        v2s = held("v2s", [P, S2], U8)
+        w2s = held("w2s", [P, PASSES * K], U8)
+
+        nc.vector.tensor_copy(v2s[:], tab_s[:].indirect(idx2[:]))
+        w1_raw = {}
+
+        def load_w1(a, b, offset):
+            t = staged("w1_raw%d%d" % (a, b), [P, PACK, KP], F32, offset)
+            nc.sync.dma_start(t[:], w1[KP * a : KP * (a + 1), KP * b : KP * (b + 1)].rearrange("(p j) c -> p j c", j=PACK))
+            w1_raw[a, b] = t
+
+        for a in range(PASSES):
+            load_w1(a, 0, (4 + a) * chunk)
+
+        def gather_v(a, q):
+            nc.vector.tensor_copy(vw[a][:, NQ * q : NQ * (q + 1)], tab_w[a][:].indirect(idx[:, 16 * q : 16 * (q + 1)]))
+
+        for q in range(QS):
+            gather_v(0, q)
+        nc.vector.tensor_copy(v2w[0][:], tab_w[0][:].indirect(idx2[:]))
+        for a in range(PASSES):
+            load_w1(a, 1, a * chunk)
+        nc.vector.tensor_copy(
+            w2s[:].rearrange("p (g i m) -> p g i m", i=PACK, m=P),
+            w2s_raw[:].rearrange("p (g m i) -> p g i m", i=PACK, m=P),
+        )
+        for q in range(QS):
+            gather_v(1, q)
+
+        w1w = held("w1w", [P, PASSES * K], U32)
+        w1s = held("w1s", [P, PASSES * K], U8)
+
+        def round_w1(a, b):
+            g = ring.tile([P, PACK * KP], BF16, name="w1_bf", align_bytes=64)
+            nc.vector.tensor_copy(
+                g[:].rearrange("p (i m j) -> p m i j", i=PACK, j=PACK),
+                w1_raw[a, b][:].rearrange("p j (m i) -> p m i j", i=PACK),
+            )
+            return g
+
+        def quantize_w1(a, b, g):
+            cols = slice(K * a + KP * b, K * a + KP * (b + 1))
+            nc.vector.quantize_mx(out=w1w[:, cols].bitcast(FP8X4), scales=w1s[:, cols], in_=g[:])
+
+        def stage1(which, b, q, banks):
+            tiles = [bank(n) for n in banks]
+            cols = slice(NQ * q, NQ * (q + 1))
+            for a in range(PASSES):
+                for i in range(PACK):
+                    c0 = K * a + KP * b + P * i
+                    if which == 1:
+                        lw, ls = w1w[:, c0 : c0 + P].bitcast(FP8X4), w1s[:, c0 : c0 + P]
+                    else:
+                        lw, ls = w2w[:, 2 * c0 : 2 * (c0 + P)].bitcast(FP4X4), w2s[:, c0 : c0 + P]
+                    nc.tensor.matmul_mx(
+                        out=tiles[i // 2][:, i % 2, :],
+                        lhsT=lw,
+                        lhsT_scale=ls,
+                        rhs=vw[a][:, cols].bitcast(FP8X4),
+                        rhs_scale=vs[a][:, cols],
+                        start=(a == 0 and i % 2 == 0),
+                        stop=(a == PASSES - 1 and i % 2 == 1),
+                    )
+            return tiles
+
+        def square(dst, tiles):
+            for u in range(2):
+                nc.scalar.activation(dst[:, u, :].rearrange("p (j e) -> p j e", e=2), tiles[u][:].rearrange("p e j -> p j e"), ACT.Square)
+
+        pairs = [(0, 1), (2, 3), (4, 5), (6, 7)]
+        sq2 = {}
+        chunks = [(0, 0), (1, 0), (0, 1), (1, 1)]
+        for b in range(PASSES):
+            for q in range(QS):
+                tiles = stage1(2, b, q, pairs[q])
+                sq2[b, q] = held("sq2_%d%d" % (b, q), [P, 2, 2 * NQ], F32)
+                square(sq2[b, q], tiles)
+        rounded = {}
+        for n in range(len(chunks) + 1):
+            if n < len(chunks):
+                rounded[n] = round_w1(*chunks[n])
+            if n >= 1:
+                quantize_w1(*chunks[n - 1], rounded[n - 1])
+        nc.vector.tensor_copy(v2w[1][:], tab_w[1][:].indirect(idx2[:]))
+
+        hw = held("hw", [P, PASSES * S], U32)
+        hs = held("hs", [P, PASSES * S], U8)
+        esq = held("esq", [P, QS, MT * NQ], F32)
+        units = [(0, 0), (0, 1), (1, 0), (1, 1), (0, 2), (1, 2), (0, 3), (1, 3)]
+        c1_banks = [0, 1, 2, 0, 1, 0, 1, 0]
+        e_banks = [3, 2, 3, 1]
+        sums = {}
+        e_tiles = {}
+
+        def front(n):
+            b, q = units[n]
+            tiles = stage1(1, b, q, pairs[c1_banks[n]])
+            sq1 = ring3.tile([P, 2, 2 * NQ], F32, name="sq1")
+            square(sq1, tiles)
+            if n == len(units) - 1:
+                total = keep.tile([P, 2, 2 * NQ], F32, name="last_total", tag="tail")
+            else:
+                total = ring3.tile([P, 2, 2 * NQ], F32, name="total", bufs=4)
+            nc.vector.tensor_tensor(total[:], sq1[:], sq2[b, q][:], ALU.add)
+            sums[n] = total
+
+        def back(n):
+            b, q = units[n]
+            h = ring.tile([P, PACK * NQ], BF16, name="h", align_bytes=64)
+            nc.scalar.activation(
+                h[:].rearrange("p (j u e) -> p j u e", u=2, e=2),
+                sums[n][:].rearrange("p u (j e) -> p j u e", e=2),
+                ACT.Sqrt,
+            )
+            cols = slice(S * b + NQ * q, S * b + NQ * (q + 1))
+            nc.vector.quantize_mx(out=hw[:, cols].bitcast(FP8X4), scales=hs[:, cols], in_=h[:])
+
+        def stage2(q):
+            tiles = [bank(n) for n in pairs[e_banks[q]]]
+            for mt in range(MT):
+                for b in range(PASSES):
+                    cols = slice(S * b + NQ * q, S * b + NQ * (q + 1))
+                    nc.tensor.matmul_mx(
+                        out=tiles[mt // 2][:, mt % 2, :],
+                        lhsT=v2w[b][:, P * mt : P * (mt + 1)].bitcast(FP8X4),
+                        lhsT_scale=v2s[4 * b :, P * mt : P * (mt + 1)],
+                        rhs=hw[:, cols].bitcast(FP8X4),
+                        rhs_scale=hs[:, cols],
+                        start=(b == 0),
+                        stop=(b == PASSES - 1),
+                    )
+            e_tiles[q] = tiles
+
+        def square_e(q):
+            tiles = e_tiles[q]
+            for u in range(2):
+                flat = tiles[u][:].rearrange("p e j -> p (e j)")
+                e = ring.tile([P, 2 * NQ], F32, name="e")
+                nc.vector.tensor_copy(e[:], flat)
+                nc.vector.tensor_tensor(esq[:, q, 2 * NQ * u : 2 * NQ * (u + 1)], flat, e[:], ALU.mult)
+
+        for n in range(len(units) + 3):
+            if n < len(units):
+                front(n)
+            if n == len(units) - 1:
+                square_e(0)
+            if 2 <= n < len(units) + 2:
+                back(n - 2)
+                if units[n - 2][0] == PASSES - 1:
+                    stage2(units[n - 2][1])
+        for q in range(1, QS):
+            square_e(q)
+
+        res = keep.tile([P, QS, MT * NQ], F32, name="res", tag="tail")
+        for q in range(QS):
+            for u in range(2):
+                cols = slice(2 * NQ * u, 2 * NQ * (u + 1))
+                nc.scalar.activation(res[:, q, cols], esq[:, q, cols], ACT.Ln, bias=1.0)
+                nc.sync.dma_start(
+                    out[2 * P * u : 2 * P * (u + 1), NQ * q : NQ * (q + 1)].rearrange("(e p) j -> p e j", p=P),
+                    res[:, q, cols].rearrange("p (e j) -> p e j", e=2),
+                )

@@ -56,6 +56,11 @@ def tile_list_gear_whine_pairs_kernel(tc, tab_words, tab_scales, offs, offs2, w1
         nc.vector.memset(w2s_raw[:].bitcast(I32), 0)
         nc.vector.memset(vs_hi[:].bitcast(I32), 0)
 
+        warm_in = held("warm_in", [P, 1], F32)
+        warm_out = held("warm_out", [P, 1], F32)
+        nc.gpsimd.memset(warm_in[:], 1.0)
+        nc.scalar.activation(warm_out[:], warm_in[:], ACT.Sqrt)
+
         w2w_raw = {}
         for b in range(PASSES):
             for a in range(PASSES):

from contextlib import ExitStack

import concourse.mybir as mybir

K, T, S, S2 = 1024, 4096, 1024, 512
FLOPS = 2 * (2 * K * K * S + K * S2 * S)

F32 = mybir.dt.float32
BF16 = mybir.dt.bfloat16
I32 = mybir.dt.int32
U32 = mybir.dt.uint32
U16 = mybir.dt.uint16
U8 = mybir.dt.uint8
FP8X4 = mybir.dt.float8_e4m3fn_x4
FP4X4 = mybir.dt.float4_e2m1fn_x4
ACT = mybir.ActivationFunctionType
ALU = mybir.AluOpType

P = 128
PACK = 4
KP = P * PACK
PASSES = K // KP
QUADS = 4
NQ = 256
QS = S // NQ
MT = S2 // P


def tile_list_gear_whine_pairs_kernel(tc, tab_words, tab_scales, offs, offs2, w1, w2_words, w2_scales, out):
    nc = tc.nc
    with ExitStack() as ctx:
        lists = ctx.enter_context(tc.tile_pool(name="lists", bufs=1))
        keep = ctx.enter_context(tc.tile_pool(name="keep", bufs=1))
        ring = ctx.enter_context(tc.tile_pool(name="ring", bufs=2))
        ring3 = ctx.enter_context(tc.tile_pool(name="ring3", bufs=3))
        stage = ctx.enter_context(tc.tile_pool(name="stage", bufs=1))
        psum = ctx.enter_context(tc.psum_pool(name="psum", bufs=1))

        def held(name, shape, dtype):
            return keep.tile(shape, dtype, name=name, align_bytes=64)

        def bank(n):
            return psum.tile([P, 2, NQ], F32, name="bank%d" % n)

        idx = lists.tile([P, S // 16], U16, name="idx")
        idx2 = lists.tile([P, S2 // 16], U16, name="idx2")
        chunk = 4 * PACK * KP

        def staged(name, shape, dtype, offset):
            return stage.tile(shape, dtype, name=name, offset=offset, align_bytes=64)

        tab_s = staged("tab_s", [P, T], U8, 5 * chunk - T // 2)
        w2s_raw = held("w2s_raw", [P, PASSES * K], U8)
        vs_hi = held("vs_hi", [P, S], U8)
        nc.vector.memset(tab_s[:].bitcast(I32), 0)
        nc.vector.memset(w2s_raw[:].bitcast(I32), 0)
        nc.vector.memset(vs_hi[:].bitcast(I32), 0)

        warm_in = held("warm_in", [P, 1], F32)
        warm_out = held("warm_out", [P, 1], F32)
        nc.gpsimd.memset(warm_in[:], 1.0)
        nc.scalar.activation(warm_out[:], warm_in[:], ACT.Sqrt)

        w2w_raw = {}
        for b in range(PASSES):
            for a in range(PASSES):
                t = staged("w2w_raw%d%d" % (a, b), [P, 2 * KP], U8, 2 * a * chunk if b == 0 else (6 * chunk + 2 * KP * a))
                nc.sync.dma_start(t[:].bitcast(I32), w2_words[a, :, 2 * KP * b : 2 * KP * (b + 1)].bitcast(I32))
                w2w_raw[a, b] = t
        nc.sync.dma_start(idx[:], offs)
        nc.sync.dma_start(idx2[:], offs2)
        for q in range(QUADS):
            nc.sync.dma_start(tab_s[32 * q : 32 * q + 8, :].bitcast(I32), tab_scales[:, 4 * q : 4 * q + 4, :].bitcast(I32))
        for q in range(QUADS):
            nc.sync.dma_start(
                w2s_raw[32 * q : 32 * q + 4, :].bitcast(I32).rearrange("r (a c) -> r a c", a=PASSES),
                w2_scales[:, 4 * q : 4 * q + 4, :].rearrange("a r c -> r a c").bitcast(I32),
            )
        w2w = held("w2w", [P, PASSES * 2 * K], U8)
        for b in range(PASSES):
            for a in range(PASSES):
                c0 = 2 * (K * a + KP * b)
                nc.scalar.copy(
                    w2w[:, c0 : c0 + 2 * KP].bitcast(U16).rearrange("p (i m) -> p i m", i=PACK),
                    w2w_raw[a, b][:].bitcast(U16).rearrange("p (m i) -> p i m", i=PACK),
                )
        tab_w = []
        for a in range(PASSES):
            t = staged("tab_w%d" % a, [P, T], U32, 2 * a * chunk)
            nc.sync.dma_start(t[:].bitcast(I32), tab_words[a].rearrange("p t i -> p (t i)").bitcast(I32))
            tab_w.append(t)
        vs_lo = held("vs_lo", [P, S], U8)
        nc.vector.tensor_copy(vs_lo[:], tab_s[:].indirect(idx[:]))
        nc.scalar.dma_start(vs_hi[0:100, :].bitcast(I32), vs_lo[4:104, :].bitcast(I32))
        vs = [vs_lo, vs_hi]
        vw = [held("vw%d" % a, [P, S], U32) for a in range(PASSES)]
        v2w = [held("v2w%d" % a, [P, S2], U32) for a in range(PASSES)]
        v2s = held("v2s", [P, S2], U8)
        w2s = held("w2s", [P, PASSES * K], U8)

        nc.vector.tensor_copy(v2s[:], tab_s[:].indirect(idx2[:]))
        w1_raw = {}

        def load_w1(a, b, offset):
            t = staged("w1_raw%d%d" % (a, b), [P, PACK, KP], F32, offset)
            nc.sync.dma_start(t[:], w1[KP * a : KP * (a + 1), KP * b : KP * (b + 1)].rearrange("(p j) c -> p j c", j=PACK))
            w1_raw[a, b] = t

        for a in range(PASSES):
            load_w1(a, 0, (4 + a) * chunk)

        def gather_v(a, q):
            nc.vector.tensor_copy(vw[a][:, NQ * q : NQ * (q + 1)], tab_w[a][:].indirect(idx[:, 16 * q : 16 * (q + 1)]))

        for q in range(QS):
            gather_v(0, q)
        nc.vector.tensor_copy(v2w[0][:], tab_w[0][:].indirect(idx2[:]))
        for a in range(PASSES):
            load_w1(a, 1, a * chunk)
        nc.vector.tensor_copy(
            w2s[:].rearrange("p (g i m) -> p g i m", i=PACK, m=P),
            w2s_raw[:].rearrange("p (g m i) -> p g i m", i=PACK, m=P),
        )
        for q in range(QS):
            gather_v(1, q)

        w1w = held("w1w", [P, PASSES * K], U32)
        w1s = held("w1s", [P, PASSES * K], U8)

        def round_w1(a, b):
            g = ring.tile([P, PACK * KP], BF16, name="w1_bf", align_bytes=64)
            nc.vector.tensor_copy(
                g[:].rearrange("p (i m j) -> p m i j", i=PACK, j=PACK),
                w1_raw[a, b][:].rearrange("p j (m i) -> p m i j", i=PACK),
            )
            return g

        def quantize_w1(a, b, g):
            cols = slice(K * a + KP * b, K * a + KP * (b + 1))
            nc.vector.quantize_mx(out=w1w[:, cols].bitcast(FP8X4), scales=w1s[:, cols], in_=g[:])

        def stage1(which, b, q, banks):
            tiles = [bank(n) for n in banks]
            cols = slice(NQ * q, NQ * (q + 1))
            for a in range(PASSES):
                for i in range(PACK):
                    c0 = K * a + KP * b + P * i
                    if which == 1:
                        lw, ls = w1w[:, c0 : c0 + P].bitcast(FP8X4), w1s[:, c0 : c0 + P]
                    else:
                        lw, ls = w2w[:, 2 * c0 : 2 * (c0 + P)].bitcast(FP4X4), w2s[:, c0 : c0 + P]
                    nc.tensor.matmul_mx(
                        out=tiles[i // 2][:, i % 2, :],
                        lhsT=lw,
                        lhsT_scale=ls,
                        rhs=vw[a][:, cols].bitcast(FP8X4),
                        rhs_scale=vs[a][:, cols],
                        start=(a == 0 and i % 2 == 0),
                        stop=(a == PASSES - 1 and i % 2 == 1),
                    )
            return tiles

        def square(dst, tiles):
            for u in range(2):
                nc.scalar.activation(dst[:, u, :].rearrange("p (j e) -> p j e", e=2), tiles[u][:].rearrange("p e j -> p j e"), ACT.Square)

        pairs = [(0, 1), (2, 3), (4, 5), (6, 7)]
        sq2 = {}
        chunks = [(0, 0), (1, 0), (0, 1), (1, 1)]
        for b in range(PASSES):
            for q in range(QS):
                tiles = stage1(2, b, q, pairs[q])
                sq2[b, q] = held("sq2_%d%d" % (b, q), [P, 2, 2 * NQ], F32)
                square(sq2[b, q], tiles)
        rounded = {}
        for n in range(len(chunks) + 1):
            if n < len(chunks):
                rounded[n] = round_w1(*chunks[n])
            if n >= 1:
                quantize_w1(*chunks[n - 1], rounded[n - 1])
        nc.vector.tensor_copy(v2w[1][:], tab_w[1][:].indirect(idx2[:]))

        hw = held("hw", [P, PASSES * S], U32)
        hs = held("hs", [P, PASSES * S], U8)
        esq = held("esq", [P, QS, MT * NQ], F32)
        units = [(0, 0), (0, 1), (1, 0), (1, 1), (0, 2), (1, 2), (0, 3), (1, 3)]
        c1_banks = [0, 1, 2, 0, 1, 0, 1, 0]
        e_banks = [3, 2, 3, 1]
        sums = {}
        e_tiles = {}

        def front(n):
            b, q = units[n]
            tiles = stage1(1, b, q, pairs[c1_banks[n]])
            sq1 = ring3.tile([P, 2, 2 * NQ], F32, name="sq1")
            square(sq1, tiles)
            if n == len(units) - 1:
                total = keep.tile([P, 2, 2 * NQ], F32, name="last_total", tag="tail")
            else:
                total = ring3.tile([P, 2, 2 * NQ], F32, name="total", bufs=4)
            nc.vector.tensor_tensor(total[:], sq1[:], sq2[b, q][:], ALU.add)
            sums[n] = total

        def back(n):
            b, q = units[n]
            h = ring.tile([P, PACK * NQ], BF16, name="h", align_bytes=64)
            nc.scalar.activation(
                h[:].rearrange("p (j u e) -> p j u e", u=2, e=2),
                sums[n][:].rearrange("p u (j e) -> p j u e", e=2),
                ACT.Sqrt,
            )
            cols = slice(S * b + NQ * q, S * b + NQ * (q + 1))
            nc.vector.quantize_mx(out=hw[:, cols].bitcast(FP8X4), scales=hs[:, cols], in_=h[:])

        def stage2(q):
            tiles = [bank(n) for n in pairs[e_banks[q]]]
            for mt in range(MT):
                for b in range(PASSES):
                    cols = slice(S * b + NQ * q, S * b + NQ * (q + 1))
                    nc.tensor.matmul_mx(
                        out=tiles[mt // 2][:, mt % 2, :],
                        lhsT=v2w[b][:, P * mt : P * (mt + 1)].bitcast(FP8X4),
                        lhsT_scale=v2s[4 * b :, P * mt : P * (mt + 1)],
                        rhs=hw[:, cols].bitcast(FP8X4),
                        rhs_scale=hs[:, cols],
                        start=(b == 0),
                        stop=(b == PASSES - 1),
                    )
            e_tiles[q] = tiles

        def square_e(q):
            tiles = e_tiles[q]
            for u in range(2):
                flat = tiles[u][:].rearrange("p e j -> p (e j)")
                e = ring.tile([P, 2 * NQ], F32, name="e")
                nc.vector.tensor_copy(e[:], flat)
                nc.vector.tensor_tensor(esq[:, q, 2 * NQ * u : 2 * NQ * (u + 1)], flat, e[:], ALU.mult)

        for n in range(len(units) + 3):
            if n < len(units):
                front(n)
            if n == len(units) - 1:
                square_e(0)
            if 2 <= n < len(units) + 2:
                back(n - 2)
                if units[n - 2][0] == PASSES - 1:
                    stage2(units[n - 2][1])
        for q in range(1, QS):
            square_e(q)

        res = keep.tile([P, QS, MT * NQ], F32, name="res", tag="tail")
        for q in range(QS):
            for u in range(2):
                cols = slice(2 * NQ * u, 2 * NQ * (u + 1))
                nc.scalar.activation(res[:, q, cols], esq[:, q, cols], ACT.Ln, bias=1.0)
                nc.sync.dma_start(
                    out[2 * P * u : 2 * P * (u + 1), NQ * q : NQ * (q + 1)].rearrange("(e p) j -> p e j", p=P),
                    res[:, q, cols].rearrange("p (e j) -> p e j", e=2),
                )
